import numpy as np
import ml_dtypes


def mxq(x, axis, fmt="e4m3"):
    dtype, down = {"e4m3": (ml_dtypes.float8_e4m3fn, 7), "e5m2": (ml_dtypes.float8_e5m2, 14)}[fmt]
    v = np.moveaxis(np.asarray(x, np.float32).astype(ml_dtypes.bfloat16).astype(np.float64), axis, -1)
    blocks = v.reshape(v.shape[:-1] + (-1, 32))
    amax = np.abs(blocks).max(-1, keepdims=True)
    byte = np.maximum(np.where(amax > 0, np.frexp(amax)[1] - 1 + 127, 0) - down, 1)
    scale = np.exp2(byte - 127.0)
    codes = (blocks / scale).astype(np.float32).astype(dtype).astype(np.float64)
    return np.moveaxis((codes * scale).reshape(v.shape), -1, axis)


WIDE = False


def mx_kscale(k):
    if not WIDE:
        return np.ones(k)
    levels = np.array([30, -30])
    if k % 512:
        return np.exp2(np.random.permutation(np.resize(levels, k // 32))).repeat(32)
    a = np.empty((k // 512, 16))
    for p in range(k // 512):
        a[p, :8] = np.random.permutation(np.resize(levels, 8))
        for g in range(8):
            far = levels[np.abs(levels - a[p, g]) >= 10]
            a[p, g + 8] = far[np.random.randint(len(far))]
    return np.exp2(a.ravel()).repeat(32)


def f64(x):
    return np.asarray(x).astype(np.float64)


def striped(idx):
    return np.tile(np.asarray(idx).reshape(-1, 16).T, (8, 1)).astype(np.uint16)


def unstriped(offs):
    return offs[:16].T.reshape(-1).astype(np.int64)


E2M1 = np.array([0.0, 0.5, 1.0, 1.5, 2.0, 3.0, 4.0, 6.0, -0.0, -0.5, -1.0, -1.5, -2.0, -3.0, -4.0, -6.0])


def pack_weight(w, fmt):
    k, n = w.shape
    w = f64(np.asarray(w, np.float32).astype(ml_dtypes.bfloat16)).reshape(k // 32, 32, n)
    amax = np.abs(w).max(1)
    if fmt == "e4m3":
        byte = np.frexp(amax)[1] - 1 + 127 - 7
    else:
        mant, ex = np.frexp(amax / 6.0)
        byte = np.where(mant > 0.5, ex, ex - 1) + 127
    byte = np.clip(np.where(amax > 0, byte, 1), 1, 254)
    scaled = (w * np.exp2(127.0 - byte)[:, None, :]).reshape(k, n).astype(np.float32)
    by_word = np.ascontiguousarray(scaled.reshape(k // 512, 128, 4, n).transpose(0, 1, 3, 2))
    if fmt == "e4m3":
        words = by_word.astype(ml_dtypes.float8_e4m3fn).view(np.uint8)
    else:
        c = by_word.astype(ml_dtypes.float4_e2m1fn).view(np.uint8) & 0xF
        words = (c[..., 0::2] | (c[..., 1::2] << 4)).reshape(k // 512, 128, 2 * n)
    return np.ascontiguousarray(words), np.ascontiguousarray(byte.astype(np.uint8).reshape(k // 512, 16, n))


def unpack_weight(words, scales, fmt):
    g, _, n = scales.shape
    words = np.ascontiguousarray(words).reshape(g, 128, n, -1)
    if fmt == "e4m3":
        vals = words.view(ml_dtypes.float8_e4m3fn).astype(np.float64)
    else:
        nib = np.empty((g, 128, n, 4), np.uint8)
        nib[..., 0::2] = words & 0xF
        nib[..., 1::2] = words >> 4
        vals = E2M1[nib]
    vals = vals * np.repeat(np.exp2(scales.astype(np.float64) - 127.0), 8, axis=1)[..., None]
    return vals.transpose(0, 1, 3, 2).reshape(g * 512, n)


K, T, J, R, G, N, Z = 512, 1024, 256, 512, 128, 256, 512


def setup_inputs():
    n = np.random.standard_normal
    idx = np.random.permutation(T)[:J]
    idx2 = np.random.permutation(T)[:J]
    idx3 = np.random.permutation(Z)[:G]
    fk = mx_kscale(K)
    fr = mx_kscale(R)
    wp = pack_weight(n((K, R)) * 1 / np.sqrt(K) * fk[:, None] * fr, "e2m1")
    wbp = pack_weight(n((R, N)) * 1 / np.sqrt(R) / fr[:, None], "e4m3")
    return {
        "xf": (n((K, T))).astype(np.float32),
        "fk": (np.random.uniform(0.5, 2.0, (K, 1)) / fk[:, None]).astype(np.float32),
        "w_words": wp[0],
        "w_scales": wp[1],
        "wb_words": wbp[0],
        "wb_scales": wbp[1],
        "tz": (n((N, Z)) * 0.6).astype(np.float32),
        "rw": (np.random.uniform(0.5, 2.0, (1, G))).astype(np.float32),
        "offs": striped(idx),
        "offs2": striped(idx2),
        "offs3": striped(idx3),
    }


def reference(xf, fk, w_words, w_scales, wb_words, wb_scales, tz, rw, offs, offs2, offs3):
    idx = unstriped(offs)
    idx2 = unstriped(offs2)
    idx3 = unstriped(offs3)
    wu = unpack_weight(w_words, w_scales, "e2m1")
    wbu = unpack_weight(wb_words, wb_scales, "e4m3")
    u = (f64(xf)[:, idx] - f64(xf)[:, idx2]) * f64(fk)
    uq = mxq(u, 0, "e4m3")
    a = wu.T @ uq
    hid = a.reshape(R, G, J // G).max(axis=2)
    hidq = mxq(hid, 0, "e5m2")
    p = wbu.T @ hidq
    y = np.maximum(p, f64(tz)[:, idx3]) * f64(rw)
    return y

@@ -1,0 +1,187 @@
+from contextlib import ExitStack
+
+import concourse.mybir as mybir
+from concourse.masks import make_identity
+
+K, T, J, R, G, N, Z = 512, 1024, 256, 512, 128, 256, 512
+FLOPS = 2 * K * R * J + 2 * R * N * G
+
+F32 = mybir.dt.float32
+BF16 = mybir.dt.bfloat16
+I32 = mybir.dt.int32
+U32 = mybir.dt.uint32
+U16 = mybir.dt.uint16
+U8 = mybir.dt.uint8
+E4M3 = mybir.dt.float8_e4m3fn_x4
+E5M2 = mybir.dt.float8_e5m2_x4
+E2M1 = mybir.dt.float4_e2m1fn_x4
+ALU = mybir.AluOpType
+COPY = mybir.ActivationFunctionType.Copy
+
+P = 128
+PACK = 4
+HALVES = 2
+JH = J // HALVES
+GH = G // HALVES
+LIST_ROWS = 16
+
+
+def load_scale_rows(nc, plane, scales):
+    for q in range(4):
+        nc.sync.dma_start(
+            out=plane[32 * q : 32 * q + 4, :].bitcast(I32),
+            in_=scales[0, 4 * q : 4 * q + 4, :].bitcast(I32),
+        )
+
+
+def tile_list_pickgaps_pooled_floored_kernel(
+    tc, xf, fk, w_words, w_scales, wb_words, wb_scales, tz, rw, offs, offs2, offs3, out
+):
+    nc = tc.nc
+    with ExitStack() as ctx:
+        sb = ctx.enter_context(tc.tile_pool(name="sb", bufs=1))
+        ps = ctx.enter_context(tc.psum_pool(name="ps", bufs=1))
+
+        w_plane_raw = sb.tile([P, R], U8, name="w_plane_raw", align_bytes=64)
+        nc.gpsimd.memset(w_plane_raw[:].bitcast(I32), 0)
+        wb_plane = sb.tile([P, N], U8, name="wb_plane", align_bytes=64)
+        nc.vector.memset(wb_plane[:].bitcast(I32), 0)
+        factor = sb.tile([P, PACK], F32, name="factor")
+        nc.gpsimd.dma_start(out=factor[:], in_=fk.rearrange("(p t) o -> p (t o)", t=PACK))
+        rw_column = sb.tile([P, 1], F32, name="rw_column")
+        nc.gpsimd.dma_start(out=rw_column[:], in_=rw.rearrange("o g -> g o"))
+
+        w_raw = sb.tile([P, 2 * R], U8, name="w_raw", align_bytes=64)
+        nc.sync.dma_start(out=w_raw[:].bitcast(I32), in_=w_words[0].bitcast(I32))
+        idx2 = sb.tile([P, J // LIST_ROWS], U16, name="idx2")
+        nc.sync.dma_start(idx2[:], offs2)
+        idx = sb.tile([P, J // LIST_ROWS], U16, name="idx")
+        nc.sync.dma_start(idx[:], offs)
+        xf_planes = xf.rearrange("(p t) c -> t p c", t=PACK)
+        x = [sb.tile([P, T], F32, name="x%d" % t) for t in range(PACK)]
+        for t in range(2):
+            nc.sync.dma_start(out=x[t][:], in_=xf_planes[t])
+        load_scale_rows(nc, w_plane_raw, w_scales)
+        for t in range(2, PACK):
+            nc.sync.dma_start(out=x[t][:], in_=xf_planes[t])
+        floor_table = sb.tile([P, N // P, Z], F32, name="floor_table")
+        nc.sync.dma_start(out=floor_table[:], in_=tz.rearrange("(c p) z -> p c z", p=P))
+        wb_codes = sb.tile([P, N], U32, name="wb_codes", align_bytes=64)
+        nc.sync.dma_start(
+            out=wb_codes[:].bitcast(I32),
+            in_=wb_words[0].rearrange("p n t -> p (n t)").bitcast(I32),
+        )
+        idx3 = sb.tile([P, G // LIST_ROWS], U16, name="idx3")
+        nc.sync.dma_start(idx3[:], offs3)
+        load_scale_rows(nc, wb_plane, wb_scales)
+
+        w_codes = sb.tile([P, 2 * R], U8, name="w_codes", align_bytes=64)
+        nc.vector.tensor_copy(
+            out=w_codes[:].bitcast(U16).rearrange("p (t m) -> p t m", t=PACK),
+            in_=w_raw[:].bitcast(U16).rearrange("p (m t) -> p t m", t=PACK),
+        )
+
+        identity = sb.tile([P, P], F32, name="identity")
+        make_identity(nc, identity[:])
+        rw_rows = ps.tile([P, G], F32, name="rw_rows")
+        nc.tensor.transpose(rw_rows[:], rw_column[:].to_broadcast([P, P]), identity[:])
+
+        u = [sb.tile([P, JH, PACK], BF16, name="u%d" % h, align_bytes=64) for h in range(HALVES)]
+        half = [slice(h * JH, (h + 1) * JH) for h in range(HALVES)]
+        whole = slice(0, J)
+
+        def picks(window, offsets, slots):
+            return window[:].indirect(offsets[:, slots.start // LIST_ROWS : slots.stop // LIST_ROWS])
+
+        def scale(t, h, gap):
+            nc.vector.tensor_scalar(
+                out=u[h][:, :, t], in0=gap[:, half[h]], scalar1=factor[:, t : t + 1], scalar2=None, op0=ALU.mult
+            )
+
+        last = PACK - 1
+        for t in range(last):
+            first = sb.tile([P, J], F32, name="first%d" % t)
+            second = sb.tile([P, J], F32, name="second%d" % t)
+            gap = sb.tile([P, J], F32, name="gap%d" % t, tag="gap%d" % t, align_bytes=64)
+            nc.scalar.activation(second[:], picks(x[t], idx2, whole), COPY)
+            if t == 1:
+                nc.scalar.activation(first[:], picks(x[t], idx, whole), COPY)
+                w_plane = sb.tile([P, R], U8, name="w_plane", tag="gap0", align_bytes=64)
+                nc.vector.tensor_copy(
+                    out=w_plane[:].rearrange("p (t m) -> p t m", t=PACK),
+                    in_=w_plane_raw[:].rearrange("p (m t) -> p t m", t=PACK),
+                )
+            else:
+                nc.vector.tensor_copy(first[:, half[0]], picks(x[t], idx, half[0]))
+                nc.scalar.activation(first[:, half[1]], picks(x[t], idx, half[1]), COPY)
+            nc.vector.tensor_tensor(gap[:], first[:], second[:], ALU.subtract)
+            for h in range(HALVES):
+                scale(t, h, gap)
+
+        first = sb.tile([P, J], F32, name="first_last")
+        second = sb.tile([P, J], F32, name="second_last")
+        gap = sb.tile([P, J], F32, name="gap_last")
+        nc.vector.tensor_copy(first[:, half[0]], picks(x[last], idx, half[0]))
+        for h in range(HALVES):
+            nc.scalar.activation(second[:, half[h]], picks(x[last], idx2, half[h]), COPY)
+        nc.scalar.activation(first[:, half[1]], picks(x[last], idx, half[1]), COPY)
+
+        a = []
+        for h in range(HALVES):
+            nc.vector.tensor_tensor(gap[:, half[h]], first[:, half[h]], second[:, half[h]], ALU.subtract)
+            scale(last, h, gap)
+            u_codes = sb.tile([P, JH], U32, name="u_codes%d" % h, align_bytes=64)
+            u_plane = sb.tile([P, JH], U8, name="u_plane%d" % h, align_bytes=64)
+            nc.vector.quantize_mx(
+                out=u_codes[:].bitcast(E4M3), scales=u_plane[:], in_=u[h][:].rearrange("p j t -> p (j t)")
+            )
+            bank = ps.tile([P, PACK, JH], F32, name="a%d" % h)
+            for t in range(PACK):
+                nc.tensor.matmul_mx(
+                    out=bank[:, t, :],
+                    lhsT=w_codes[:, 2 * P * t : 2 * P * (t + 1)].bitcast(E2M1),
+                    lhsT_scale=w_plane[:, P * t : P * (t + 1)],
+                    rhs=u_codes[:].bitcast(E4M3),
+                    rhs_scale=u_plane[:],
+                    start=True,
+                    stop=True,
+                )
+            a.append(bank)
+
+        floor = sb.tile([P, N // P, G], F32, name="floor")
+        for c in range(N // P):
+            nc.scalar.activation(floor[:, c, :], floor_table[:, c, :].indirect(idx3[:]), COPY)
+
+        hid = sb.tile([P, G, PACK], BF16, name="hid", align_bytes=64)
+        for h in range(HALVES):
+            nc.vector.tensor_reduce(
+                out=hid[:, h * GH : (h + 1) * GH, :],
+                in_=a[h][:].rearrange("p t (g e) -> p g t e", e=2),
+                axis=mybir.AxisListType.X,
+                op=ALU.max,
+            )
+        hid_codes = sb.tile([P, G], U32, name="hid_codes", align_bytes=64)
+        hid_plane = sb.tile([P, G], U8, name="hid_plane", align_bytes=64)
+        nc.vector.quantize_mx(
+            out=hid_codes[:].bitcast(E5M2), scales=hid_plane[:], in_=hid[:].rearrange("p g t -> p (g t)")
+        )
+
+        floored = []
+        for c in range(N // P):
+            product = ps.tile([P, G], F32, name="product%d" % c)
+            nc.tensor.matmul_mx(
+                out=product[:],
+                lhsT=wb_codes[:, P * c : P * (c + 1)].bitcast(E4M3),
+                lhsT_scale=wb_plane[:, P * c : P * (c + 1)],
+                rhs=hid_codes[:].bitcast(E5M2),
+                rhs_scale=hid_plane[:],
+                start=True,
+                stop=True,
+            )
+            raised = sb.tile([P, G], F32, name="raised%d" % c)
+            nc.vector.tensor_tensor(raised[:], product[:], floor[:, c, :], ALU.max)
+            floored.append(raised)
+        for c, queue in enumerate((nc.sync, nc.scalar)):
+            y = sb.tile([P, G], F32, name="y%d" % c)
+            nc.vector.tensor_tensor(y[:], floored[c][:], rw_rows[:], ALU.mult)
+            queue.dma_start(out=out[P * c : P * (c + 1), :], in_=y[:])

@@ -44,12 +44,13 @@ def tile_list_pickgaps_pooled_floored_kernel(
 
         w_plane_raw = sb.tile([P, R], U8, name="w_plane_raw", align_bytes=64)
         nc.gpsimd.memset(w_plane_raw[:].bitcast(I32), 0)
+        seed = sb.tile([P, 1], F32, name="seed")
+        nc.gpsimd.memset(seed[:], 0.0)
+        warm = sb.tile([P, 1], F32, name="warm")
+        nc.scalar.activation(warm[:], seed[:], COPY)
+
         wb_plane = sb.tile([P, N], U8, name="wb_plane", align_bytes=64)
         nc.vector.memset(wb_plane[:].bitcast(I32), 0)
-        factor = sb.tile([P, PACK], F32, name="factor")
-        nc.gpsimd.dma_start(out=factor[:], in_=fk.rearrange("(p t) o -> p (t o)", t=PACK))
-        rw_column = sb.tile([P, 1], F32, name="rw_column")
-        nc.gpsimd.dma_start(out=rw_column[:], in_=rw.rearrange("o g -> g o"))
 
         w_raw = sb.tile([P, 2 * R], U8, name="w_raw", align_bytes=64)
         nc.sync.dma_start(out=w_raw[:].bitcast(I32), in_=w_words[0].bitcast(I32))
@@ -59,11 +60,15 @@ def tile_list_pickgaps_pooled_floored_kernel(
         nc.sync.dma_start(idx[:], offs)
         xf_planes = xf.rearrange("(p t) c -> t p c", t=PACK)
         x = [sb.tile([P, T], F32, name="x%d" % t) for t in range(PACK)]
-        for t in range(2):
-            nc.sync.dma_start(out=x[t][:], in_=xf_planes[t])
+        nc.sync.dma_start(out=x[0][:], in_=xf_planes[0])
+        factor = sb.tile([P, PACK], F32, name="factor")
+        nc.sync.dma_start(out=factor[:], in_=fk.rearrange("(p t) o -> p (t o)", t=PACK))
+        nc.sync.dma_start(out=x[1][:], in_=xf_planes[1])
         load_scale_rows(nc, w_plane_raw, w_scales)
         for t in range(2, PACK):
             nc.sync.dma_start(out=x[t][:], in_=xf_planes[t])
+        rw_column = sb.tile([P, 1], F32, name="rw_column")
+        nc.sync.dma_start(out=rw_column[:], in_=rw.rearrange("o g -> g o"))
         floor_table = sb.tile([P, N // P, Z], F32, name="floor_table")
         nc.sync.dma_start(out=floor_table[:], in_=tz.rearrange("(c p) z -> p c z", p=P))
         wb_codes = sb.tile([P, N], U32, name="wb_codes", align_bytes=64)
@@ -88,48 +93,40 @@ def tile_list_pickgaps_pooled_floored_kernel(
 
         u = [sb.tile([P, JH, PACK], BF16, name="u%d" % h, align_bytes=64) for h in range(HALVES)]
         half = [slice(h * JH, (h + 1) * JH) for h in range(HALVES)]
-        whole = slice(0, J)
 
         def picks(window, offsets, slots):
             return window[:].indirect(offsets[:, slots.start // LIST_ROWS : slots.stop // LIST_ROWS])
 
         def scale(t, h, gap):
             nc.vector.tensor_scalar(
-                out=u[h][:, :, t], in0=gap[:, half[h]], scalar1=factor[:, t : t + 1], scalar2=None, op0=ALU.mult
+                out=u[h][:, :, t], in0=gap, scalar1=factor[:, t : t + 1], scalar2=None, op0=ALU.mult
             )
 
+        def half_tiles(kind, t):
+            names = ["%s%d_%d" % (kind, t, h) for h in range(HALVES)]
+            return [sb.tile([P, JH], F32, name=name, tag=name, align_bytes=64) for name in names]
+
         last = PACK - 1
-        for t in range(last):
-            first = sb.tile([P, J], F32, name="first%d" % t)
-            second = sb.tile([P, J], F32, name="second%d" % t)
-            gap = sb.tile([P, J], F32, name="gap%d" % t, tag="gap%d" % t, align_bytes=64)
-            nc.scalar.activation(second[:], picks(x[t], idx2, whole), COPY)
+        for t in range(PACK):
+            second = half_tiles("second", t)
+            gap = half_tiles("gap", t)
+            first = sb.tile([P, JH], F32, name="first%d" % t)
+            for h in range(HALVES):
+                nc.scalar.activation(second[h][:], picks(x[t], idx2, half[h]), COPY)
+            nc.scalar.activation(first[:], picks(x[t], idx, half[1]), COPY)
             if t == 1:
-                nc.scalar.activation(first[:], picks(x[t], idx, whole), COPY)
-                w_plane = sb.tile([P, R], U8, name="w_plane", tag="gap0", align_bytes=64)
+                w_plane = sb.tile([P, R], U8, name="w_plane", tag="gap0_1", align_bytes=64)
                 nc.vector.tensor_copy(
                     out=w_plane[:].rearrange("p (t m) -> p t m", t=PACK),
                     in_=w_plane_raw[:].rearrange("p (m t) -> p t m", t=PACK),
                 )
-            else:
-                nc.vector.tensor_copy(first[:, half[0]], picks(x[t], idx, half[0]))
-                nc.scalar.activation(first[:, half[1]], picks(x[t], idx, half[1]), COPY)
-            nc.vector.tensor_tensor(gap[:], first[:], second[:], ALU.subtract)
-            for h in range(HALVES):
-                scale(t, h, gap)
-
-        first = sb.tile([P, J], F32, name="first_last")
-        second = sb.tile([P, J], F32, name="second_last")
-        gap = sb.tile([P, J], F32, name="gap_last")
-        nc.vector.tensor_copy(first[:, half[0]], picks(x[last], idx, half[0]))
-        for h in range(HALVES):
-            nc.scalar.activation(second[:, half[h]], picks(x[last], idx2, half[h]), COPY)
-        nc.scalar.activation(first[:, half[1]], picks(x[last], idx, half[1]), COPY)
+            nc.vector.tensor_tensor(gap[0][:], picks(x[t], idx, half[0]), second[0][:], ALU.subtract)
+            scale(t, 0, gap[0][:])
+            nc.vector.tensor_tensor(gap[1][:], first[:], second[1][:], ALU.subtract)
+            scale(t, 1, gap[1][:])
 
         a = []
         for h in range(HALVES):
-            nc.vector.tensor_tensor(gap[:, half[h]], first[:, half[h]], second[:, half[h]], ALU.subtract)
-            scale(last, h, gap)
             u_codes = sb.tile([P, JH], U32, name="u_codes%d" % h, align_bytes=64)
             u_plane = sb.tile([P, JH], U8, name="u_plane%d" % h, align_bytes=64)
             nc.vector.quantize_mx(
@@ -148,9 +145,11 @@ def tile_list_pickgaps_pooled_floored_kernel(
                 )
             a.append(bank)
 
-        floor = sb.tile([P, N // P, G], F32, name="floor")
+        floor = []
         for c in range(N // P):
-            nc.scalar.activation(floor[:, c, :], floor_table[:, c, :].indirect(idx3[:]), COPY)
+            picked = sb.tile([P, G], F32, name="floor%d" % c, tag="second%d_%d" % (last, c), align_bytes=64)
+            nc.scalar.activation(picked[:], floor_table[:, c, :].indirect(idx3[:]), COPY)
+            floor.append(picked)
 
         hid = sb.tile([P, G, PACK], BF16, name="hid", align_bytes=64)
         for h in range(HALVES):
@@ -179,7 +178,7 @@ def tile_list_pickgaps_pooled_floored_kernel(
                 stop=True,
             )
             raised = sb.tile([P, G], F32, name="raised%d" % c)
-            nc.vector.tensor_tensor(raised[:], product[:], floor[:, c, :], ALU.max)
+            nc.vector.tensor_tensor(raised[:], product[:], floor[c][:], ALU.max)
             floored.append(raised)
         for c, queue in enumerate((nc.sync, nc.scalar)):
             y = sb.tile([P, G], F32, name="y%d" % c)

@@ -20,18 +20,25 @@ COPY = mybir.ActivationFunctionType.Copy
 
 P = 128
 PACK = 4
+QUADRANTS = 4
 HALVES = 2
 JH = J // HALVES
 GH = G // HALVES
 LIST_ROWS = 16
+MX_ALIGN = 64
 
 
-def load_scale_rows(nc, plane, scales):
-    for q in range(4):
+def load_scale_rows(nc, scale_tile, scales):
+    for q in range(QUADRANTS):
         nc.sync.dma_start(
-            out=plane[32 * q : 32 * q + 4, :].bitcast(I32),
+            out=scale_tile[32 * q : 32 * q + 4, :].bitcast(I32),
             in_=scales[0, 4 * q : 4 * q + 4, :].bitcast(I32),
         )
+
+
+def picks(window, offsets, h):
+    columns = JH // LIST_ROWS
+    return window[:].indirect(offsets[:, h * columns : (h + 1) * columns])
 
 
 def tile_list_pickgaps_pooled_floored_kernel(
@@ -42,48 +49,46 @@ def tile_list_pickgaps_pooled_floored_kernel(
         sb = ctx.enter_context(tc.tile_pool(name="sb", bufs=1))
         ps = ctx.enter_context(tc.psum_pool(name="ps", bufs=1))
 
-        w_plane_raw = sb.tile([P, R], U8, name="w_plane_raw", align_bytes=64)
-        nc.gpsimd.memset(w_plane_raw[:].bitcast(I32), 0)
-        seed = sb.tile([P, 1], F32, name="seed")
-        nc.gpsimd.memset(seed[:], 0.0)
-        warm = sb.tile([P, 1], F32, name="warm")
-        nc.scalar.activation(warm[:], seed[:], COPY)
+        w_scales_raw = sb.tile([P, R], U8, name="w_scales_raw", align_bytes=MX_ALIGN)
+        nc.gpsimd.memset(w_scales_raw[:].bitcast(I32), 0)
+        wb_scale = sb.tile([P, N], U8, name="wb_scale", align_bytes=MX_ALIGN)
+        nc.vector.memset(wb_scale[:].bitcast(I32), 0)
 
-        wb_plane = sb.tile([P, N], U8, name="wb_plane", align_bytes=64)
-        nc.vector.memset(wb_plane[:].bitcast(I32), 0)
+        warm_up = sb.tile([P, 1], F32, name="warm_up")
+        nc.scalar.activation(warm_up[:], wb_scale[:, 0:4].bitcast(F32), COPY)
 
-        w_raw = sb.tile([P, 2 * R], U8, name="w_raw", align_bytes=64)
-        nc.sync.dma_start(out=w_raw[:].bitcast(I32), in_=w_words[0].bitcast(I32))
+        w_words_raw = sb.tile([P, 2 * R], U8, name="w_words_raw", align_bytes=MX_ALIGN)
+        nc.sync.dma_start(out=w_words_raw[:].bitcast(I32), in_=w_words[0].bitcast(I32))
         idx2 = sb.tile([P, J // LIST_ROWS], U16, name="idx2")
         nc.sync.dma_start(idx2[:], offs2)
         idx = sb.tile([P, J // LIST_ROWS], U16, name="idx")
         nc.sync.dma_start(idx[:], offs)
-        xf_planes = xf.rearrange("(p t) c -> t p c", t=PACK)
+        xf_rows = xf.rearrange("(p t) c -> t p c", t=PACK)
         x = [sb.tile([P, T], F32, name="x%d" % t) for t in range(PACK)]
-        nc.sync.dma_start(out=x[0][:], in_=xf_planes[0])
+        nc.sync.dma_start(out=x[0][:], in_=xf_rows[0])
         factor = sb.tile([P, PACK], F32, name="factor")
         nc.sync.dma_start(out=factor[:], in_=fk.rearrange("(p t) o -> p (t o)", t=PACK))
-        nc.sync.dma_start(out=x[1][:], in_=xf_planes[1])
-        load_scale_rows(nc, w_plane_raw, w_scales)
+        nc.sync.dma_start(out=x[1][:], in_=xf_rows[1])
+        load_scale_rows(nc, w_scales_raw, w_scales)
         for t in range(2, PACK):
-            nc.sync.dma_start(out=x[t][:], in_=xf_planes[t])
+            nc.sync.dma_start(out=x[t][:], in_=xf_rows[t])
         rw_column = sb.tile([P, 1], F32, name="rw_column")
         nc.sync.dma_start(out=rw_column[:], in_=rw.rearrange("o g -> g o"))
-        floor_table = sb.tile([P, N // P, Z], F32, name="floor_table")
-        nc.sync.dma_start(out=floor_table[:], in_=tz.rearrange("(c p) z -> p c z", p=P))
-        wb_codes = sb.tile([P, N], U32, name="wb_codes", align_bytes=64)
+        tz_rows = sb.tile([P, N // P, Z], F32, name="tz_rows")
+        nc.sync.dma_start(out=tz_rows[:], in_=tz.rearrange("(c p) z -> p c z", p=P))
+        wb_codes = sb.tile([P, N], U32, name="wb_codes", align_bytes=MX_ALIGN)
         nc.sync.dma_start(
             out=wb_codes[:].bitcast(I32),
             in_=wb_words[0].rearrange("p n t -> p (n t)").bitcast(I32),
         )
         idx3 = sb.tile([P, G // LIST_ROWS], U16, name="idx3")
         nc.sync.dma_start(idx3[:], offs3)
-        load_scale_rows(nc, wb_plane, wb_scales)
+        load_scale_rows(nc, wb_scale, wb_scales)
 
-        w_codes = sb.tile([P, 2 * R], U8, name="w_codes", align_bytes=64)
+        w_codes = sb.tile([P, 2 * R], U8, name="w_codes", align_bytes=MX_ALIGN)
         nc.vector.tensor_copy(
             out=w_codes[:].bitcast(U16).rearrange("p (t m) -> p t m", t=PACK),
-            in_=w_raw[:].bitcast(U16).rearrange("p (m t) -> p t m", t=PACK),
+            in_=w_words_raw[:].bitcast(U16).rearrange("p (m t) -> p t m", t=PACK),
         )
 
         identity = sb.tile([P, P], F32, name="identity")
@@ -91,78 +96,75 @@ def tile_list_pickgaps_pooled_floored_kernel(
         rw_rows = ps.tile([P, G], F32, name="rw_rows")
         nc.tensor.transpose(rw_rows[:], rw_column[:].to_broadcast([P, P]), identity[:])
 
-        u = [sb.tile([P, JH, PACK], BF16, name="u%d" % h, align_bytes=64) for h in range(HALVES)]
-        half = [slice(h * JH, (h + 1) * JH) for h in range(HALVES)]
-
-        def picks(window, offsets, slots):
-            return window[:].indirect(offsets[:, slots.start // LIST_ROWS : slots.stop // LIST_ROWS])
-
-        def scale(t, h, gap):
-            nc.vector.tensor_scalar(
-                out=u[h][:, :, t], in0=gap, scalar1=factor[:, t : t + 1], scalar2=None, op0=ALU.mult
-            )
-
         def half_tiles(kind, t):
             names = ["%s%d_%d" % (kind, t, h) for h in range(HALVES)]
-            return [sb.tile([P, JH], F32, name=name, tag=name, align_bytes=64) for name in names]
+            return [sb.tile([P, JH], F32, name=name, tag=name, align_bytes=MX_ALIGN) for name in names]
 
-        last = PACK - 1
+        u = [sb.tile([P, JH, PACK], BF16, name="u%d" % h, align_bytes=MX_ALIGN) for h in range(HALVES)]
+
+        def scale_and_round(t, h, gap_tile):
+            nc.vector.tensor_scalar(
+                out=u[h][:, :, t], in0=gap_tile[:], scalar1=factor[:, t : t + 1], scalar2=None, op0=ALU.mult
+            )
+
         for t in range(PACK):
             second = half_tiles("second", t)
             gap = half_tiles("gap", t)
-            first = sb.tile([P, JH], F32, name="first%d" % t)
+            first_of_half_1 = sb.tile([P, JH], F32, name="first%d" % t)
             for h in range(HALVES):
-                nc.scalar.activation(second[h][:], picks(x[t], idx2, half[h]), COPY)
-            nc.scalar.activation(first[:], picks(x[t], idx, half[1]), COPY)
+                nc.scalar.activation(second[h][:], picks(x[t], idx2, h), COPY)
+            nc.scalar.activation(first_of_half_1[:], picks(x[t], idx, 1), COPY)
             if t == 1:
-                w_plane = sb.tile([P, R], U8, name="w_plane", tag="gap0_1", align_bytes=64)
+                w_scale = sb.tile([P, R], U8, name="w_scale", tag="gap0_1", align_bytes=MX_ALIGN)
                 nc.vector.tensor_copy(
-                    out=w_plane[:].rearrange("p (t m) -> p t m", t=PACK),
-                    in_=w_plane_raw[:].rearrange("p (m t) -> p t m", t=PACK),
+                    out=w_scale[:].rearrange("p (t m) -> p t m", t=PACK),
+                    in_=w_scales_raw[:].rearrange("p (m t) -> p t m", t=PACK),
                 )
-            nc.vector.tensor_tensor(gap[0][:], picks(x[t], idx, half[0]), second[0][:], ALU.subtract)
-            scale(t, 0, gap[0][:])
-            nc.vector.tensor_tensor(gap[1][:], first[:], second[1][:], ALU.subtract)
-            scale(t, 1, gap[1][:])
+            nc.vector.tensor_tensor(gap[0][:], picks(x[t], idx, 0), second[0][:], ALU.subtract)
+            scale_and_round(t, 0, gap[0])
+            nc.vector.tensor_tensor(gap[1][:], first_of_half_1[:], second[1][:], ALU.subtract)
+            scale_and_round(t, 1, gap[1])
 
         a = []
         for h in range(HALVES):
-            u_codes = sb.tile([P, JH], U32, name="u_codes%d" % h, align_bytes=64)
-            u_plane = sb.tile([P, JH], U8, name="u_plane%d" % h, align_bytes=64)
+            u_codes = sb.tile([P, JH], U32, name="u_codes%d" % h, align_bytes=MX_ALIGN)
+            u_scale = sb.tile([P, JH], U8, name="u_scale%d" % h, align_bytes=MX_ALIGN)
             nc.vector.quantize_mx(
-                out=u_codes[:].bitcast(E4M3), scales=u_plane[:], in_=u[h][:].rearrange("p j t -> p (j t)")
+                out=u_codes[:].bitcast(E4M3), scales=u_scale[:], in_=u[h][:].rearrange("p j t -> p (j t)")
             )
-            bank = ps.tile([P, PACK, JH], F32, name="a%d" % h)
+            banks = [ps.tile([P, 2, JH], F32, name="a%d_%d" % (h, s)) for s in range(PACK // 2)]
             for t in range(PACK):
                 nc.tensor.matmul_mx(
-                    out=bank[:, t, :],
+                    out=banks[t // 2][:, t % 2, :],
                     lhsT=w_codes[:, 2 * P * t : 2 * P * (t + 1)].bitcast(E2M1),
-                    lhsT_scale=w_plane[:, P * t : P * (t + 1)],
+                    lhsT_scale=w_scale[:, P * t : P * (t + 1)],
                     rhs=u_codes[:].bitcast(E4M3),
-                    rhs_scale=u_plane[:],
+                    rhs_scale=u_scale[:],
                     start=True,
                     stop=True,
                 )
-            a.append(bank)
+            a.append(banks)
 
         floor = []
         for c in range(N // P):
-            picked = sb.tile([P, G], F32, name="floor%d" % c, tag="second%d_%d" % (last, c), align_bytes=64)
-            nc.scalar.activation(picked[:], floor_table[:, c, :].indirect(idx3[:]), COPY)
+            tag = "second%d_%d" % (PACK - 1, c)
+            picked = sb.tile([P, G], F32, name="floor%d" % c, tag=tag, align_bytes=MX_ALIGN)
+            nc.scalar.activation(picked[:], tz_rows[:, c, :].indirect(idx3[:]), COPY)
             floor.append(picked)
 
-        hid = sb.tile([P, G, PACK], BF16, name="hid", align_bytes=64)
+        hid = sb.tile([P, G, PACK], BF16, name="hid", align_bytes=MX_ALIGN)
         for h in range(HALVES):
-            nc.vector.tensor_reduce(
-                out=hid[:, h * GH : (h + 1) * GH, :],
-                in_=a[h][:].rearrange("p t (g e) -> p g t e", e=2),
-                axis=mybir.AxisListType.X,
-                op=ALU.max,
-            )
-        hid_codes = sb.tile([P, G], U32, name="hid_codes", align_bytes=64)
-        hid_plane = sb.tile([P, G], U8, name="hid_plane", align_bytes=64)
+            for s in range(PACK // 2):
+                nc.vector.tensor_reduce(
+                    out=hid[:, h * GH : (h + 1) * GH, 2 * s : 2 * s + 2],
+                    in_=a[h][s][:].rearrange("p i (g e) -> p g i e", e=2),
+                    axis=mybir.AxisListType.X,
+                    op=ALU.max,
+                )
+        hid_codes = sb.tile([P, G], U32, name="hid_codes", align_bytes=MX_ALIGN)
+        hid_scale = sb.tile([P, G], U8, name="hid_scale", align_bytes=MX_ALIGN)
         nc.vector.quantize_mx(
-            out=hid_codes[:].bitcast(E5M2), scales=hid_plane[:], in_=hid[:].rearrange("p g t -> p (g t)")
+            out=hid_codes[:].bitcast(E5M2), scales=hid_scale[:], in_=hid[:].rearrange("p g t -> p (g t)")
         )
 
         floored = []
@@ -171,9 +173,9 @@ def tile_list_pickgaps_pooled_floored_kernel(
             nc.tensor.matmul_mx(
                 out=product[:],
                 lhsT=wb_codes[:, P * c : P * (c + 1)].bitcast(E4M3),
-                lhsT_scale=wb_plane[:, P * c : P * (c + 1)],
+                lhsT_scale=wb_scale[:, P * c : P * (c + 1)],
                 rhs=hid_codes[:].bitcast(E5M2),
-                rhs_scale=hid_plane[:],
+                rhs_scale=hid_scale[:],
                 start=True,
                 stop=True,
             )

from contextlib import ExitStack

import concourse.mybir as mybir
from concourse.masks import make_identity

K, T, J, R, G, N, Z = 512, 1024, 256, 512, 128, 256, 512
FLOPS = 2 * K * R * J + 2 * R * N * G

F32 = mybir.dt.float32
BF16 = mybir.dt.bfloat16
I32 = mybir.dt.int32
U32 = mybir.dt.uint32
U16 = mybir.dt.uint16
U8 = mybir.dt.uint8
E4M3 = mybir.dt.float8_e4m3fn_x4
E5M2 = mybir.dt.float8_e5m2_x4
E2M1 = mybir.dt.float4_e2m1fn_x4
ALU = mybir.AluOpType
COPY = mybir.ActivationFunctionType.Copy

P = 128
PACK = 4
QUADRANTS = 4
HALVES = 2
JH = J // HALVES
GH = G // HALVES
LIST_ROWS = 16
MX_ALIGN = 64


def load_scale_rows(nc, scale_tile, scales):
    for q in range(QUADRANTS):
        nc.sync.dma_start(
            out=scale_tile[32 * q : 32 * q + 4, :].bitcast(I32),
            in_=scales[0, 4 * q : 4 * q + 4, :].bitcast(I32),
        )


def picks(window, offsets, h):
    columns = JH // LIST_ROWS
    return window[:].indirect(offsets[:, h * columns : (h + 1) * columns])


def tile_list_pickgaps_pooled_floored_kernel(
    tc, xf, fk, w_words, w_scales, wb_words, wb_scales, tz, rw, offs, offs2, offs3, out
):
    nc = tc.nc
    with ExitStack() as ctx:
        sb = ctx.enter_context(tc.tile_pool(name="sb", bufs=1))
        ps = ctx.enter_context(tc.psum_pool(name="ps", bufs=1))

        w_scales_raw = sb.tile([P, R], U8, name="w_scales_raw", align_bytes=MX_ALIGN)
        nc.gpsimd.memset(w_scales_raw[:].bitcast(I32), 0)
        wb_scale = sb.tile([P, N], U8, name="wb_scale", align_bytes=MX_ALIGN)
        nc.vector.memset(wb_scale[:].bitcast(I32), 0)

        warm_up = sb.tile([P, 1], F32, name="warm_up")
        nc.scalar.activation(warm_up[:], wb_scale[:, 0:4].bitcast(F32), COPY)

        w_words_raw = sb.tile([P, 2 * R], U8, name="w_words_raw", align_bytes=MX_ALIGN)
        nc.sync.dma_start(out=w_words_raw[:].bitcast(I32), in_=w_words[0].bitcast(I32))
        idx2 = sb.tile([P, J // LIST_ROWS], U16, name="idx2")
        nc.sync.dma_start(idx2[:], offs2)
        idx = sb.tile([P, J // LIST_ROWS], U16, name="idx")
        nc.sync.dma_start(idx[:], offs)
        xf_rows = xf.rearrange("(p t) c -> t p c", t=PACK)
        x = [sb.tile([P, T], F32, name="x%d" % t) for t in range(PACK)]
        nc.sync.dma_start(out=x[0][:], in_=xf_rows[0])
        factor = sb.tile([P, PACK], F32, name="factor")
        nc.sync.dma_start(out=factor[:], in_=fk.rearrange("(p t) o -> p (t o)", t=PACK))
        nc.sync.dma_start(out=x[1][:], in_=xf_rows[1])
        load_scale_rows(nc, w_scales_raw, w_scales)
        for t in range(2, PACK):
            nc.sync.dma_start(out=x[t][:], in_=xf_rows[t])
        rw_column = sb.tile([P, 1], F32, name="rw_column")
        nc.sync.dma_start(out=rw_column[:], in_=rw.rearrange("o g -> g o"))
        tz_rows = sb.tile([P, N // P, Z], F32, name="tz_rows")
        nc.sync.dma_start(out=tz_rows[:], in_=tz.rearrange("(c p) z -> p c z", p=P))
        wb_codes = sb.tile([P, N], U32, name="wb_codes", align_bytes=MX_ALIGN)
        nc.sync.dma_start(
            out=wb_codes[:].bitcast(I32),
            in_=wb_words[0].rearrange("p n t -> p (n t)").bitcast(I32),
        )
        idx3 = sb.tile([P, G // LIST_ROWS], U16, name="idx3")
        nc.sync.dma_start(idx3[:], offs3)
        load_scale_rows(nc, wb_scale, wb_scales)

        w_codes = sb.tile([P, 2 * R], U8, name="w_codes", align_bytes=MX_ALIGN)
        nc.vector.tensor_copy(
            out=w_codes[:].bitcast(U16).rearrange("p (t m) -> p t m", t=PACK),
            in_=w_words_raw[:].bitcast(U16).rearrange("p (m t) -> p t m", t=PACK),
        )

        identity = sb.tile([P, P], F32, name="identity")
        make_identity(nc, identity[:])
        rw_rows = ps.tile([P, G], F32, name="rw_rows")
        nc.tensor.transpose(rw_rows[:], rw_column[:].to_broadcast([P, P]), identity[:])

        def half_tiles(kind, t):
            names = ["%s%d_%d" % (kind, t, h) for h in range(HALVES)]
            return [sb.tile([P, JH], F32, name=name, tag=name, align_bytes=MX_ALIGN) for name in names]

        u = [sb.tile([P, JH, PACK], BF16, name="u%d" % h, align_bytes=MX_ALIGN) for h in range(HALVES)]

        def scale_and_round(t, h, gap_tile):
            nc.vector.tensor_scalar(
                out=u[h][:, :, t], in0=gap_tile[:], scalar1=factor[:, t : t + 1], scalar2=None, op0=ALU.mult
            )

        for t in range(PACK):
            second = half_tiles("second", t)
            gap = half_tiles("gap", t)
            first_of_half_1 = sb.tile([P, JH], F32, name="first%d" % t)
            for h in range(HALVES):
                nc.scalar.activation(second[h][:], picks(x[t], idx2, h), COPY)
            nc.scalar.activation(first_of_half_1[:], picks(x[t], idx, 1), COPY)
            if t == 1:
                w_scale = sb.tile([P, R], U8, name="w_scale", tag="gap0_1", align_bytes=MX_ALIGN)
                nc.vector.tensor_copy(
                    out=w_scale[:].rearrange("p (t m) -> p t m", t=PACK),
                    in_=w_scales_raw[:].rearrange("p (m t) -> p t m", t=PACK),
                )
            nc.vector.tensor_tensor(gap[0][:], picks(x[t], idx, 0), second[0][:], ALU.subtract)
            scale_and_round(t, 0, gap[0])
            nc.vector.tensor_tensor(gap[1][:], first_of_half_1[:], second[1][:], ALU.subtract)
            scale_and_round(t, 1, gap[1])

        a = []
        for h in range(HALVES):
            u_codes = sb.tile([P, JH], U32, name="u_codes%d" % h, align_bytes=MX_ALIGN)
            u_scale = sb.tile([P, JH], U8, name="u_scale%d" % h, align_bytes=MX_ALIGN)
            nc.vector.quantize_mx(
                out=u_codes[:].bitcast(E4M3), scales=u_scale[:], in_=u[h][:].rearrange("p j t -> p (j t)")
            )
            banks = [ps.tile([P, 2, JH], F32, name="a%d_%d" % (h, s)) for s in range(PACK // 2)]
            for t in range(PACK):
                nc.tensor.matmul_mx(
                    out=banks[t // 2][:, t % 2, :],
                    lhsT=w_codes[:, 2 * P * t : 2 * P * (t + 1)].bitcast(E2M1),
                    lhsT_scale=w_scale[:, P * t : P * (t + 1)],
                    rhs=u_codes[:].bitcast(E4M3),
                    rhs_scale=u_scale[:],
                    start=True,
                    stop=True,
                )
            a.append(banks)

        floor = []
        for c in range(N // P):
            tag = "second%d_%d" % (PACK - 1, c)
            picked = sb.tile([P, G], F32, name="floor%d" % c, tag=tag, align_bytes=MX_ALIGN)
            nc.scalar.activation(picked[:], tz_rows[:, c, :].indirect(idx3[:]), COPY)
            floor.append(picked)

        hid = sb.tile([P, G, PACK], BF16, name="hid", align_bytes=MX_ALIGN)
        for h in range(HALVES):
            for s in range(PACK // 2):
                nc.vector.tensor_reduce(
                    out=hid[:, h * GH : (h + 1) * GH, 2 * s : 2 * s + 2],
                    in_=a[h][s][:].rearrange("p i (g e) -> p g i e", e=2),
                    axis=mybir.AxisListType.X,
                    op=ALU.max,
                )
        hid_codes = sb.tile([P, G], U32, name="hid_codes", align_bytes=MX_ALIGN)
        hid_scale = sb.tile([P, G], U8, name="hid_scale", align_bytes=MX_ALIGN)
        nc.vector.quantize_mx(
            out=hid_codes[:].bitcast(E5M2), scales=hid_scale[:], in_=hid[:].rearrange("p g t -> p (g t)")
        )

        floored = []
        for c in range(N // P):
            product = ps.tile([P, G], F32, name="product%d" % c)
            nc.tensor.matmul_mx(
                out=product[:],
                lhsT=wb_codes[:, P * c : P * (c + 1)].bitcast(E4M3),
                lhsT_scale=wb_scale[:, P * c : P * (c + 1)],
                rhs=hid_codes[:].bitcast(E5M2),
                rhs_scale=hid_scale[:],
                start=True,
                stop=True,
            )
            raised = sb.tile([P, G], F32, name="raised%d" % c)
            nc.vector.tensor_tensor(raised[:], product[:], floor[c][:], ALU.max)
            floored.append(raised)
        for c, queue in enumerate((nc.sync, nc.scalar)):
            y = sb.tile([P, G], F32, name="y%d" % c)
            nc.vector.tensor_tensor(y[:], floored[c][:], rw_rows[:], ALU.mult)
            queue.dma_start(out=out[P * c : P * (c + 1), :], in_=y[:])
